import numpy as np
import ml_dtypes


def mxq(x, axis, fmt="e4m3"):
    dtype, down = {"e4m3": (ml_dtypes.float8_e4m3fn, 7), "e5m2": (ml_dtypes.float8_e5m2, 14)}[fmt]
    v = np.moveaxis(np.asarray(x, np.float32).astype(ml_dtypes.bfloat16).astype(np.float64), axis, -1)
    blocks = v.reshape(v.shape[:-1] + (-1, 32))
    amax = np.abs(blocks).max(-1, keepdims=True)
    byte = np.maximum(np.where(amax > 0, np.frexp(amax)[1] - 1 + 127, 0) - down, 1)
    scale = np.exp2(byte - 127.0)
    codes = (blocks / scale).astype(np.float32).astype(dtype).astype(np.float64)
    return np.moveaxis((codes * scale).reshape(v.shape), -1, axis)


WIDE = False


def mx_kscale(k):
    if not WIDE:
        return np.ones(k)
    levels = np.array([30, -30])
    if k % 512:
        return np.exp2(np.random.permutation(np.resize(levels, k // 32))).repeat(32)
    a = np.empty((k // 512, 16))
    for p in range(k // 512):
        a[p, :8] = np.random.permutation(np.resize(levels, 8))
        for g in range(8):
            far = levels[np.abs(levels - a[p, g]) >= 10]
            a[p, g + 8] = far[np.random.randint(len(far))]
    return np.exp2(a.ravel()).repeat(32)


def f64(x):
    return np.asarray(x).astype(np.float64)


def striped(idx):
    return np.tile(np.asarray(idx).reshape(-1, 16).T, (8, 1)).astype(np.uint16)


def unstriped(offs):
    return offs[:16].T.reshape(-1).astype(np.int64)


E2M1 = np.array([0.0, 0.5, 1.0, 1.5, 2.0, 3.0, 4.0, 6.0, -0.0, -0.5, -1.0, -1.5, -2.0, -3.0, -4.0, -6.0])


def pack_weight(w, fmt):
    k, n = w.shape
    w = f64(np.asarray(w, np.float32).astype(ml_dtypes.bfloat16)).reshape(k // 32, 32, n)
    amax = np.abs(w).max(1)
    if fmt in ("e4m3", "e5m2"):
        byte = np.frexp(amax)[1] - 1 + 127 - (7 if fmt == "e4m3" else 14)
    else:
        mant, ex = np.frexp(amax / 6.0)
        byte = np.where(mant > 0.5, ex, ex - 1) + 127
    byte = np.clip(np.where(amax > 0, byte, 1), 1, 254)
    scaled = (w * np.exp2(127.0 - byte)[:, None, :]).reshape(k, n).astype(np.float32)
    by_word = np.ascontiguousarray(scaled.reshape(k // 512, 128, 4, n).transpose(0, 1, 3, 2))
    if fmt in ("e4m3", "e5m2"):
        words = by_word.astype(ml_dtypes.float8_e4m3fn if fmt == "e4m3" else ml_dtypes.float8_e5m2).view(np.uint8)
    else:
        c = by_word.astype(ml_dtypes.float4_e2m1fn).view(np.uint8) & 0xF
        words = (c[..., 0::2] | (c[..., 1::2] << 4)).reshape(k // 512, 128, 2 * n)
    return np.ascontiguousarray(words), np.ascontiguousarray(byte.astype(np.uint8).reshape(k // 512, 16, n))


def unpack_weight(words, scales, fmt):
    g, _, n = scales.shape
    words = np.ascontiguousarray(words).reshape(g, 128, n, -1)
    if fmt in ("e4m3", "e5m2"):
        vals = words.view(ml_dtypes.float8_e4m3fn if fmt == "e4m3" else ml_dtypes.float8_e5m2).astype(np.float64)
    else:
        nib = np.empty((g, 128, n, 4), np.uint8)
        nib[..., 0::2] = words & 0xF
        nib[..., 1::2] = words >> 4
        vals = E2M1[nib]
    vals = vals * np.repeat(np.exp2(scales.astype(np.float64) - 127.0), 8, axis=1)[..., None]
    return vals.transpose(0, 1, 3, 2).reshape(g * 512, n)


K, T, J, R, C, O, N, L, E = 512, 1024, 256, 512, 512, 256, 256, 512, 1024


def setup_inputs():
    n = np.random.standard_normal
    idx = np.random.permutation(T)[:J]
    idx2 = np.random.permutation(C)[:J]
    idx3 = np.random.permutation(C)[:J]
    idx4 = np.random.permutation(C)[:O]
    idx5 = np.random.permutation(E)[:O]
    fk = mx_kscale(K)
    fr = mx_kscale(R)
    fl = mx_kscale(L)
    xtp = pack_weight(n((K, T)) / fk[:, None], "e2m1")
    wp = pack_weight(n((K, R)) * 1 / np.sqrt(K) * fk[:, None] * fr, "e5m2")
    w2p = pack_weight(n((K, R)) * 1 / np.sqrt(K) * fk[:, None] * fr, "e4m3")
    wbp = pack_weight(n((R, N)) * 1 / np.sqrt(R) / fr[:, None], "e4m3")
    sxp = pack_weight(n((L, O)) / fl[:, None], "e5m2")
    wsp = pack_weight(n((L, N)) * 1 / np.sqrt(L) * fl[:, None], "e4m3")
    return {
        "xt_words": xtp[0],
        "xt_scales": xtp[1],
        "w_words": wp[0],
        "w_scales": wp[1],
        "w2_words": w2p[0],
        "w2_scales": w2p[1],
        "wb_words": wbp[0],
        "wb_scales": wbp[1],
        "sx_words": sxp[0],
        "sx_scales": sxp[1],
        "ws_words": wsp[0],
        "ws_scales": wsp[1],
        "tz": (n((N, E))).astype(np.float32),
        "offs": striped(idx),
        "offs2": striped(idx2),
        "offs3": striped(idx3),
        "offs4": striped(idx4),
        "offs5": striped(idx5),
    }


def reference(xt_words, xt_scales, w_words, w_scales, w2_words, w2_scales, wb_words, wb_scales, sx_words, sx_scales, ws_words, ws_scales, tz, offs, offs2, offs3, offs4, offs5):
    idx = unstriped(offs)
    idx2 = unstriped(offs2)
    idx3 = unstriped(offs3)
    idx4 = unstriped(offs4)
    idx5 = unstriped(offs5)
    xtu = unpack_weight(xt_words, xt_scales, "e2m1")
    wu = unpack_weight(w_words, w_scales, "e5m2")
    w2u = unpack_weight(w2_words, w2_scales, "e4m3")
    wbu = unpack_weight(wb_words, wb_scales, "e4m3")
    sxu = unpack_weight(sx_words, sx_scales, "e5m2")
    wsu = unpack_weight(ws_words, ws_scales, "e4m3")
    xtidxg = xtu[:, idx]
    a = wu.T @ xtidxg
    b = w2u.T @ xtidxg
    pw = np.zeros((R, C))
    pw[:, idx2] = a
    pv = np.zeros((R, C))
    pv[:, idx3] = b
    pg = pw + pv
    hid = pg[:, idx4]
    hidq = mxq(hid, 0, "e5m2")
    p = wbu.T @ hidq + wsu.T @ sxu
    y = p + f64(tz)[:, idx5]
    return y

@@ -1,0 +1,165 @@
+from contextlib import ExitStack
+
+import concourse.mybir as mybir
+
+K, T, J, R, C, O, N, L, E = 512, 1024, 256, 512, 512, 256, 256, 512, 1024
+FLOPS = 2 * (2 * K * R * J + R * N * O + L * N * O)
+
+F32 = mybir.dt.float32
+BF16 = mybir.dt.bfloat16
+I32 = mybir.dt.int32
+U32 = mybir.dt.uint32
+U16 = mybir.dt.uint16
+U8 = mybir.dt.uint8
+E2M1 = mybir.dt.float4_e2m1fn_x4
+E4M3 = mybir.dt.float8_e4m3fn_x4
+E5M2 = mybir.dt.float8_e5m2_x4
+COPY = mybir.ActivationFunctionType.Copy
+ADD = mybir.AluOpType.add
+
+P = 128
+PACK = 4
+
+
+def tile_list_twow_shared_skip_tabled_kernel(
+    tc, xt_words, xt_scales, w_words, w_scales, w2_words, w2_scales, wb_words, wb_scales,
+    sx_words, sx_scales, ws_words, ws_scales, tz, offs, offs2, offs3, offs4, offs5, out,
+):
+    nc = tc.nc
+    with ExitStack() as ctx:
+        sb = ctx.enter_context(tc.tile_pool(name="sb", bufs=1))
+        ps = ctx.enter_context(tc.psum_pool(name="ps", bufs=1))
+
+        def load_list(src, name):
+            tile = sb.tile([P, 16], U16, name=name)
+            nc.sync.dma_start(tile[:], src)
+            return tile
+
+        def zeroed_plane(width, name):
+            plane = sb.tile([P, width], U8, name=name, align_bytes=64)
+            nc.gpsimd.memset(plane[:].bitcast(I32), 0)
+            return plane
+
+        def load_plane(plane, scales, queues):
+            rows = scales[0].bitcast(I32)
+            for q in range(4):
+                queues[q % len(queues)].dma_start(
+                    plane[32 * q : 32 * q + 4, :].bitcast(I32), rows[4 * q : 4 * q + 4, :])
+
+        def load_words(words, width, name, queue):
+            tile = sb.tile([P, width], U32, name=name, align_bytes=64)
+            queue.dma_start(tile[:].bitcast(I32), words[0].rearrange("p n t -> p (n t)").bitcast(I32))
+            return tile
+
+        xt_plane = zeroed_plane(T, "xt_plane")
+        w_plane = zeroed_plane(R, "w_plane")
+        w2_plane = zeroed_plane(R, "w2_plane")
+        ws_plane = zeroed_plane(N, "ws_plane")
+        sx_plane = zeroed_plane(O, "sx_plane")
+        wb_plane = zeroed_plane(N, "wb_plane")
+
+        list1 = load_list(offs, "list1")
+        load_plane(xt_plane, xt_scales, [nc.scalar, nc.sync])
+        xt_tile = sb.tile([P, T], U16, name="xt_tile", align_bytes=64)
+        nc.scalar.dma_start(xt_tile[:].bitcast(I32), xt_words[0].bitcast(I32))
+        w_tile = load_words(w_words, R, "w_tile", nc.sync)
+        load_plane(w_plane, w_scales, [nc.sync])
+        w2_tile = load_words(w2_words, R, "w2_tile", nc.sync)
+        load_plane(w2_plane, w2_scales, [nc.sync])
+        list2 = load_list(offs2, "list2")
+        list3 = load_list(offs3, "list3")
+        list4 = load_list(offs4, "list4")
+        list5 = load_list(offs5, "list5")
+        tz_tiles = []
+        for u in range(N // P):
+            tile = sb.tile([P, E], F32, name="tz%d" % u)
+            nc.sync.dma_start(tile[:], tz[u * P : (u + 1) * P, :])
+            tz_tiles.append(tile)
+        ws_tile = load_words(ws_words, N, "ws_tile", nc.sync)
+        sx_tile = load_words(sx_words, O, "sx_tile", nc.sync)
+        wb_tile = load_words(wb_words, N, "wb_tile", nc.sync)
+        load_plane(ws_plane, ws_scales, [nc.sync])
+        load_plane(sx_plane, sx_scales, [nc.sync])
+        load_plane(wb_plane, wb_scales, [nc.sync])
+
+        pw = [sb.tile([P, C], F32, name="pw%d" % t) for t in range(PACK)]
+        pv = [sb.tile([P, C], F32, name="pv%d" % t) for t in range(PACK)]
+        for page in pw + pv:
+            nc.vector.memset(page[:], 0.0)
+
+        xg_words = sb.tile([P, J], U16, name="xg_words", align_bytes=64)
+        xg_plane = sb.tile([P, J], U8, name="xg_plane", align_bytes=64)
+        nc.vector.tensor_copy(xg_words[:], xt_tile[:].indirect(list1[:]))
+        nc.vector.tensor_copy(xg_plane[:], xt_plane[:].indirect(list1[:]))
+
+        def first_stage(words, plane, fmt, name):
+            dealt_words = sb.tile([P, PACK, P], U32, name=name + "_dw", align_bytes=64)
+            dealt_plane = sb.tile([P, PACK, P], U8, name=name + "_dp", align_bytes=64)
+            nc.scalar.copy(
+                dealt_words[:].rearrange("p t (c i) -> p c t i", i=4),
+                words[:].rearrange("p (c i t) -> p c t i", i=4, t=PACK))
+            nc.vector.tensor_copy(dealt_plane[:], plane[:].rearrange("p (m t) -> p t m", t=PACK))
+            banks = []
+            for h in range(2):
+                bank = ps.tile([P, 2, J], F32, name="%s_bank%d" % (name, h))
+                for i in range(2):
+                    t = 2 * h + i
+                    nc.tensor.matmul_mx(
+                        out=bank[:, i, :], lhsT=dealt_words[:, t, :].bitcast(fmt), lhsT_scale=dealt_plane[:, t, :],
+                        rhs=xg_words[:].bitcast(E2M1), rhs_scale=xg_plane[:], start=True, stop=True)
+                banks.append(bank)
+            return banks
+
+        a_banks = first_stage(w_tile, w_plane, E5M2, "a")
+        b_banks = first_stage(w2_tile, w2_plane, E4M3, "b")
+
+        out_banks = []
+        for u in range(N // P):
+            bank = ps.tile([P, O], F32, name="out_bank%d" % u)
+            cols = slice(u * P, (u + 1) * P)
+            nc.tensor.matmul_mx(
+                out=bank[:], lhsT=ws_tile[:, cols].bitcast(E4M3), lhsT_scale=ws_plane[:, cols],
+                rhs=sx_tile[:].bitcast(E5M2), rhs_scale=sx_plane[:], start=True, stop=False)
+            out_banks.append(bank)
+
+        a_sb = [sb.tile([P, 2, J], F32, name="a_sb%d" % h) for h in range(2)]
+        b_sb = [sb.tile([P, 2, J], F32, name="b_sb%d" % h) for h in range(2)]
+        nc.vector.tensor_copy(a_sb[0][:], a_banks[0][:])
+        nc.scalar.copy(a_sb[1][:], a_banks[1][:])
+        nc.scalar.copy(b_sb[0][:], b_banks[0][:])
+        nc.scalar.copy(b_sb[1][:], b_banks[1][:])
+
+        hid = sb.tile([P, PACK, O], F32, name="hid")
+        pg = []
+        for t in range(PACK):
+            nc.vector.tensor_copy(pw[t][:].indirect(list2[:]), a_sb[t // 2][:, t % 2, :])
+            nc.scalar.activation(pv[t][:].indirect(list3[:]), b_sb[t // 2][:, t % 2, :], COPY)
+        for t in range(PACK - 1):
+            board = sb.tile([P, C], F32, name="pg%d" % t, tag="pg%d" % t)
+            nc.gpsimd.tensor_tensor(board[:], pw[t][:], pv[t][:], ADD)
+            pg.append(board)
+        for t in range(2):
+            nc.vector.tensor_copy(hid[:, t, :], pg[t][:].indirect(list4[:]))
+        nc.scalar.activation(hid[:, 2, :], pg[2][:].indirect(list4[:]), COPY)
+        board = sb.tile([P, C], F32, name="pg3", tag="pg1")
+        nc.vector.tensor_tensor(board[:], pw[3][:], pv[3][:], ADD)
+        nc.vector.tensor_copy(hid[:, 3, :], board[:].indirect(list4[:]))
+
+        grouped = sb.tile([P, O, PACK], BF16, name="grouped", align_bytes=64)
+        nc.vector.tensor_copy(
+            grouped[:].rearrange("p (c i) t -> p c t i", i=4), hid[:].rearrange("p t (c i) -> p c t i", i=4))
+        hid_words = sb.tile([P, O], U32, name="hid_words", align_bytes=64)
+        hid_plane = sb.tile([P, O], U8, name="hid_plane", align_bytes=64)
+        nc.vector.quantize_mx(
+            out=hid_words[:].bitcast(E5M2), scales=hid_plane[:], in_=grouped[:].rearrange("p o t -> p (o t)"))
+
+        picked = sb.tile([P, N // P, O], F32, name="picked", tag="pg2")
+        for u in range(N // P):
+            cols = slice(u * P, (u + 1) * P)
+            nc.scalar.activation(picked[:, u, :], tz_tiles[u][:].indirect(list5[:]), COPY)
+            nc.tensor.matmul_mx(
+                out=out_banks[u][:], lhsT=wb_tile[:, cols].bitcast(E4M3), lhsT_scale=wb_plane[:, cols],
+                rhs=hid_words[:].bitcast(E5M2), rhs_scale=hid_plane[:], start=False, stop=True)
+            result = sb.tile([P, O], F32, name="result%d" % u)
+            nc.vector.tensor_tensor(result[:], out_banks[u][:], picked[:, u, :], ADD)
+            (nc.sync if u == 0 else nc.scalar).dma_start(out[cols, :], result[:])

@@ -36,7 +36,7 @@ def tile_list_twow_shared_skip_tabled_kernel(
             return tile
 
         def zeroed_plane(width, name):
-            plane = sb.tile([P, width], U8, name=name, align_bytes=64)
+            plane = sb.tile([P, width], U8, name=name, tag=name, align_bytes=64)
             nc.gpsimd.memset(plane[:].bitcast(I32), 0)
             return plane
 
@@ -54,20 +54,28 @@ def tile_list_twow_shared_skip_tabled_kernel(
         xt_plane = zeroed_plane(T, "xt_plane")
         w_plane = zeroed_plane(R, "w_plane")
         w2_plane = zeroed_plane(R, "w2_plane")
-        ws_plane = zeroed_plane(N, "ws_plane")
-        sx_plane = zeroed_plane(O, "sx_plane")
-        wb_plane = zeroed_plane(N, "wb_plane")
 
         list1 = load_list(offs, "list1")
-        load_plane(xt_plane, xt_scales, [nc.scalar, nc.sync])
+        load_plane(xt_plane, xt_scales, [nc.scalar, nc.sync, nc.scalar, nc.sync])
         xt_tile = sb.tile([P, T], U16, name="xt_tile", align_bytes=64)
         nc.scalar.dma_start(xt_tile[:].bitcast(I32), xt_words[0].bitcast(I32))
         w_tile = load_words(w_words, R, "w_tile", nc.sync)
-        load_plane(w_plane, w_scales, [nc.sync])
+        load_plane(w_plane, w_scales, [nc.scalar, nc.sync, nc.sync, nc.sync])
         w2_tile = load_words(w2_words, R, "w2_tile", nc.sync)
         load_plane(w2_plane, w2_scales, [nc.sync])
         list2 = load_list(offs2, "list2")
         list3 = load_list(offs3, "list3")
+
+        pw = [sb.tile([P, C], F32, name="pw%d" % t) for t in range(3)]
+        pv = [sb.tile([P, C], F32, name="pv%d" % t) for t in range(2)]
+        for page in pw:
+            nc.vector.memset(page[:], 0.0)
+        for page in pv:
+            nc.gpsimd.memset(page[:], 0.0)
+        ws_plane = zeroed_plane(N, "ws_plane")
+        sx_plane = zeroed_plane(O, "sx_plane")
+        wb_plane = zeroed_plane(N, "wb_plane")
+
         list4 = load_list(offs4, "list4")
         list5 = load_list(offs5, "list5")
         tz_tiles = []
@@ -82,84 +90,104 @@ def tile_list_twow_shared_skip_tabled_kernel(
         load_plane(sx_plane, sx_scales, [nc.sync])
         load_plane(wb_plane, wb_scales, [nc.sync])
 
-        pw = [sb.tile([P, C], F32, name="pw%d" % t) for t in range(PACK)]
-        pv = [sb.tile([P, C], F32, name="pv%d" % t) for t in range(PACK)]
-        for page in pw + pv:
-            nc.vector.memset(page[:], 0.0)
-
         xg_words = sb.tile([P, J], U16, name="xg_words", align_bytes=64)
         xg_plane = sb.tile([P, J], U8, name="xg_plane", align_bytes=64)
         nc.vector.tensor_copy(xg_words[:], xt_tile[:].indirect(list1[:]))
         nc.vector.tensor_copy(xg_plane[:], xt_plane[:].indirect(list1[:]))
 
-        def first_stage(words, plane, fmt, name):
+        def deal(words, plane, name):
             dealt_words = sb.tile([P, PACK, P], U32, name=name + "_dw", align_bytes=64)
             dealt_plane = sb.tile([P, PACK, P], U8, name=name + "_dp", align_bytes=64)
             nc.scalar.copy(
                 dealt_words[:].rearrange("p t (c i) -> p c t i", i=4),
                 words[:].rearrange("p (c i t) -> p c t i", i=4, t=PACK))
             nc.vector.tensor_copy(dealt_plane[:], plane[:].rearrange("p (m t) -> p t m", t=PACK))
-            banks = []
-            for h in range(2):
-                bank = ps.tile([P, 2, J], F32, name="%s_bank%d" % (name, h))
-                for i in range(2):
-                    t = 2 * h + i
-                    nc.tensor.matmul_mx(
-                        out=bank[:, i, :], lhsT=dealt_words[:, t, :].bitcast(fmt), lhsT_scale=dealt_plane[:, t, :],
-                        rhs=xg_words[:].bitcast(E2M1), rhs_scale=xg_plane[:], start=True, stop=True)
-                banks.append(bank)
-            return banks
+            return dealt_words, dealt_plane
 
-        a_banks = first_stage(w_tile, w_plane, E5M2, "a")
-        b_banks = first_stage(w2_tile, w2_plane, E4M3, "b")
+        dealt = [deal(w_tile, w_plane, "a"), deal(w2_tile, w2_plane, "b")]
+        formats = [E5M2, E4M3]
 
-        out_banks = []
-        for u in range(N // P):
-            bank = ps.tile([P, O], F32, name="out_bank%d" % u)
-            cols = slice(u * P, (u + 1) * P)
+        def first_stage(dst, m, t):
             nc.tensor.matmul_mx(
-                out=bank[:], lhsT=ws_tile[:, cols].bitcast(E4M3), lhsT_scale=ws_plane[:, cols],
-                rhs=sx_tile[:].bitcast(E5M2), rhs_scale=sx_plane[:], start=True, stop=False)
+                out=dst, lhsT=dealt[m][0][:, t, :].bitcast(formats[m]), lhsT_scale=dealt[m][1][:, t, :],
+                rhs=xg_words[:].bitcast(E2M1), rhs_scale=xg_plane[:], start=True, stop=True)
+
+        a_banks = [ps.tile([P, 2, J], F32, name="a_bank%d" % h) for h in range(2)]
+        b_lone = [ps.tile([P, J], F32, name="b_lone%d" % t) for t in range(2)]
+        b_bank = ps.tile([P, 2, J], F32, name="b_bank")
+        for t in range(2):
+            first_stage(a_banks[0][:, t, :], 0, t)
+        for t in range(2):
+            first_stage(b_lone[t][:], 1, t)
+        for t in range(2):
+            first_stage(a_banks[1][:, t, :], 0, 2 + t)
+        for t in range(2):
+            first_stage(b_bank[:, t, :], 1, 2 + t)
+
+        H = O // 2
+        out_banks = []
+        for h in range(2):
+            bank = ps.tile([P, N // P, H], F32, name="out_bank%d" % h)
+            reads = slice(h * H, (h + 1) * H)
+            for u in range(N // P):
+                cols = slice(u * P, (u + 1) * P)
+                nc.tensor.matmul_mx(
+                    out=bank[:, u, :], lhsT=ws_tile[:, cols].bitcast(E4M3), lhsT_scale=ws_plane[:, cols],
+                    rhs=sx_tile[:, reads].bitcast(E5M2), rhs_scale=sx_plane[:, reads], start=(u == 0), stop=False)
             out_banks.append(bank)
 
-        a_sb = [sb.tile([P, 2, J], F32, name="a_sb%d" % h) for h in range(2)]
+        a_sb = [
+            sb.tile([P, 2, J], F32, name="a_sb0", tag="w2_plane", align_bytes=64),
+            sb.tile([P, 2, J], F32, name="a_sb1"),
+        ]
         b_sb = [sb.tile([P, 2, J], F32, name="b_sb%d" % h) for h in range(2)]
-        nc.vector.tensor_copy(a_sb[0][:], a_banks[0][:])
-        nc.scalar.copy(a_sb[1][:], a_banks[1][:])
-        nc.scalar.copy(b_sb[0][:], b_banks[0][:])
-        nc.scalar.copy(b_sb[1][:], b_banks[1][:])
+        for h in range(2):
+            nc.vector.tensor_copy(a_sb[h][:], a_banks[h][:])
+        for t in range(2):
+            nc.scalar.copy(b_sb[0][:, t, :], b_lone[t][:])
 
         hid = sb.tile([P, PACK, O], F32, name="hid")
         pg = []
         for t in range(PACK):
-            nc.vector.tensor_copy(pw[t][:].indirect(list2[:]), a_sb[t // 2][:, t % 2, :])
-            nc.scalar.activation(pv[t][:].indirect(list3[:]), b_sb[t // 2][:, t % 2, :], COPY)
-        for t in range(PACK - 1):
-            board = sb.tile([P, C], F32, name="pg%d" % t, tag="pg%d" % t)
-            nc.gpsimd.tensor_tensor(board[:], pw[t][:], pv[t][:], ADD)
-            pg.append(board)
+            nc.vector.tensor_copy(pw[t % 3][:].indirect(list2[:]), a_sb[t // 2][:, t % 2, :])
+            nc.scalar.activation(pv[t % 2][:].indirect(list3[:]), b_sb[t // 2][:, t % 2, :], COPY)
+            if t == 0:
+                nc.scalar.copy(b_sb[1][:], b_bank[:])
+            if t < PACK - 1:
+                board = sb.tile([P, C], F32, name="pg%d" % t, tag="pg%d" % t)
+                nc.gpsimd.tensor_tensor(board[:], pw[t % 3][:], pv[t % 2][:], ADD)
+                pg.append(board)
         for t in range(2):
             nc.vector.tensor_copy(hid[:, t, :], pg[t][:].indirect(list4[:]))
         nc.scalar.activation(hid[:, 2, :], pg[2][:].indirect(list4[:]), COPY)
         board = sb.tile([P, C], F32, name="pg3", tag="pg1")
-        nc.vector.tensor_tensor(board[:], pw[3][:], pv[3][:], ADD)
-        nc.vector.tensor_copy(hid[:, 3, :], board[:].indirect(list4[:]))
+        nc.vector.tensor_tensor(board[:], pw[0][:], pv[1][:], ADD)
+        nc.vector.tensor_copy(hid[:, 3, :H], board[:].indirect(list4[:, :8]))
+        nc.scalar.activation(hid[:, 3, H:], board[:].indirect(list4[:, 8:]), COPY)
 
-        grouped = sb.tile([P, O, PACK], BF16, name="grouped", align_bytes=64)
-        nc.vector.tensor_copy(
-            grouped[:].rearrange("p (c i) t -> p c t i", i=4), hid[:].rearrange("p t (c i) -> p c t i", i=4))
-        hid_words = sb.tile([P, O], U32, name="hid_words", align_bytes=64)
-        hid_plane = sb.tile([P, O], U8, name="hid_plane", align_bytes=64)
-        nc.vector.quantize_mx(
-            out=hid_words[:].bitcast(E5M2), scales=hid_plane[:], in_=grouped[:].rearrange("p o t -> p (o t)"))
-
-        picked = sb.tile([P, N // P, O], F32, name="picked", tag="pg2")
+        picked = sb.tile([P, N // P, O], F32, name="picked", tag="pg1")
         for u in range(N // P):
-            cols = slice(u * P, (u + 1) * P)
             nc.scalar.activation(picked[:, u, :], tz_tiles[u][:].indirect(list5[:]), COPY)
-            nc.tensor.matmul_mx(
-                out=out_banks[u][:], lhsT=wb_tile[:, cols].bitcast(E4M3), lhsT_scale=wb_plane[:, cols],
-                rhs=hid_words[:].bitcast(E5M2), rhs_scale=hid_plane[:], start=False, stop=True)
-            result = sb.tile([P, O], F32, name="result%d" % u)
-            nc.vector.tensor_tensor(result[:], out_banks[u][:], picked[:, u, :], ADD)
-            (nc.sync if u == 0 else nc.scalar).dma_start(out[cols, :], result[:])
+
+        grouped = [sb.tile([P, H, PACK], BF16, name="grouped%d" % h, align_bytes=64) for h in range(2)]
+        for h in range(2):
+            nc.vector.tensor_copy(
+                grouped[h][:].rearrange("p (c i) t -> p c t i", i=4),
+                hid[:, :, h * H : (h + 1) * H].rearrange("p t (c i) -> p c t i", i=4))
+        hid_words = [sb.tile([P, H], U32, name="hid_words%d" % h, align_bytes=64) for h in range(2)]
+        hid_plane = [sb.tile([P, H], U8, name="hid_plane%d" % h, align_bytes=64) for h in range(2)]
+        for h in range(2):
+            nc.vector.quantize_mx(
+                out=hid_words[h][:].bitcast(E5M2), scales=hid_plane[h][:],
+                in_=grouped[h][:].rearrange("p o t -> p (o t)"))
+        out_view = out.rearrange("(u p) o -> p u o", p=P)
+        for h in range(2):
+            reads = slice(h * H, (h + 1) * H)
+            for u in range(N // P):
+                cols = slice(u * P, (u + 1) * P)
+                nc.tensor.matmul_mx(
+                    out=out_banks[h][:, u, :], lhsT=wb_tile[:, cols].bitcast(E4M3), lhsT_scale=wb_plane[:, cols],
+                    rhs=hid_words[h][:].bitcast(E5M2), rhs_scale=hid_plane[h][:], start=False, stop=(u == N // P - 1))
+            result = sb.tile([P, N // P, H], F32, name="result%d" % h)
+            nc.vector.tensor_tensor(result[:], out_banks[h][:], picked[:, :, reads], ADD)
+            (nc.sync if h == 0 else nc.scalar).dma_start(out_view[:, :, reads], result[:])

@@ -68,10 +68,8 @@ def tile_list_twow_shared_skip_tabled_kernel(
 
         pw = [sb.tile([P, C], F32, name="pw%d" % t) for t in range(3)]
         pv = [sb.tile([P, C], F32, name="pv%d" % t) for t in range(2)]
-        for page in pw:
+        for page in pw + pv:
             nc.vector.memset(page[:], 0.0)
-        for page in pv:
-            nc.gpsimd.memset(page[:], 0.0)
         ws_plane = zeroed_plane(N, "ws_plane")
         sx_plane = zeroed_plane(O, "sx_plane")
         wb_plane = zeroed_plane(N, "wb_plane")
@@ -136,23 +134,24 @@ def tile_list_twow_shared_skip_tabled_kernel(
                     rhs=sx_tile[:, reads].bitcast(E5M2), rhs_scale=sx_plane[:, reads], start=(u == 0), stop=False)
             out_banks.append(bank)
 
-        a_sb = [
-            sb.tile([P, 2, J], F32, name="a_sb0", tag="w2_plane", align_bytes=64),
-            sb.tile([P, 2, J], F32, name="a_sb1"),
-        ]
-        b_sb = [sb.tile([P, 2, J], F32, name="b_sb%d" % h) for h in range(2)]
+        a_sb = sb.tile([P, PACK, J], F32, name="a_sb", tag="w2_plane", align_bytes=64)
         for h in range(2):
-            nc.vector.tensor_copy(a_sb[h][:], a_banks[h][:])
-        for t in range(2):
-            nc.scalar.copy(b_sb[0][:, t, :], b_lone[t][:])
+            nc.vector.tensor_copy(a_sb[:, 2 * h : 2 * h + 2, :], a_banks[h][:])
+        b_first = sb.tile([P, J], F32, name="b_first", tag="b_shared")
+        b_second = sb.tile([P, J], F32, name="b_second")
+        nc.scalar.copy(b_first[:], b_lone[0][:])
+        nc.scalar.copy(b_second[:], b_lone[1][:])
+        b_sums = [b_first[:], b_second[:]]
 
         hid = sb.tile([P, PACK, O], F32, name="hid")
         pg = []
         for t in range(PACK):
-            nc.vector.tensor_copy(pw[t % 3][:].indirect(list2[:]), a_sb[t // 2][:, t % 2, :])
-            nc.scalar.activation(pv[t % 2][:].indirect(list3[:]), b_sb[t // 2][:, t % 2, :], COPY)
+            nc.vector.tensor_copy(pw[t % 3][:].indirect(list2[:]), a_sb[:, t, :])
+            nc.scalar.activation(pv[t % 2][:].indirect(list3[:]), b_sums[t], COPY)
             if t == 0:
-                nc.scalar.copy(b_sb[1][:], b_bank[:])
+                b_rest = sb.tile([P, 2, J], F32, name="b_rest", tag="b_shared")
+                nc.scalar.copy(b_rest[:], b_bank[:])
+                b_sums.extend([b_rest[:, 0, :], b_rest[:, 1, :]])
             if t < PACK - 1:
                 board = sb.tile([P, C], F32, name="pg%d" % t, tag="pg%d" % t)
                 nc.gpsimd.tensor_tensor(board[:], pw[t % 3][:], pv[t % 2][:], ADD)

from contextlib import ExitStack

import concourse.mybir as mybir

K, T, J, R, C, O, N, L, E = 512, 1024, 256, 512, 512, 256, 256, 512, 1024
FLOPS = 2 * (2 * K * R * J + R * N * O + L * N * O)

F32 = mybir.dt.float32
BF16 = mybir.dt.bfloat16
I32 = mybir.dt.int32
U32 = mybir.dt.uint32
U16 = mybir.dt.uint16
U8 = mybir.dt.uint8
E2M1 = mybir.dt.float4_e2m1fn_x4
E4M3 = mybir.dt.float8_e4m3fn_x4
E5M2 = mybir.dt.float8_e5m2_x4
COPY = mybir.ActivationFunctionType.Copy
ADD = mybir.AluOpType.add

P = 128
PACK = 4


def tile_list_twow_shared_skip_tabled_kernel(
    tc, xt_words, xt_scales, w_words, w_scales, w2_words, w2_scales, wb_words, wb_scales,
    sx_words, sx_scales, ws_words, ws_scales, tz, offs, offs2, offs3, offs4, offs5, out,
):
    nc = tc.nc
    with ExitStack() as ctx:
        sb = ctx.enter_context(tc.tile_pool(name="sb", bufs=1))
        ps = ctx.enter_context(tc.psum_pool(name="ps", bufs=1))

        def load_list(src, name):
            tile = sb.tile([P, 16], U16, name=name)
            nc.sync.dma_start(tile[:], src)
            return tile

        def zeroed_plane(width, name):
            plane = sb.tile([P, width], U8, name=name, tag=name, align_bytes=64)
            nc.gpsimd.memset(plane[:].bitcast(I32), 0)
            return plane

        def load_plane(plane, scales, queues):
            rows = scales[0].bitcast(I32)
            for q in range(4):
                queues[q % len(queues)].dma_start(
                    plane[32 * q : 32 * q + 4, :].bitcast(I32), rows[4 * q : 4 * q + 4, :])

        def load_words(words, width, name, queue):
            tile = sb.tile([P, width], U32, name=name, align_bytes=64)
            queue.dma_start(tile[:].bitcast(I32), words[0].rearrange("p n t -> p (n t)").bitcast(I32))
            return tile

        xt_plane = zeroed_plane(T, "xt_plane")
        w_plane = zeroed_plane(R, "w_plane")
        w2_plane = zeroed_plane(R, "w2_plane")

        list1 = load_list(offs, "list1")
        load_plane(xt_plane, xt_scales, [nc.scalar, nc.sync, nc.scalar, nc.sync])
        xt_tile = sb.tile([P, T], U16, name="xt_tile", align_bytes=64)
        nc.scalar.dma_start(xt_tile[:].bitcast(I32), xt_words[0].bitcast(I32))
        w_tile = load_words(w_words, R, "w_tile", nc.sync)
        load_plane(w_plane, w_scales, [nc.scalar, nc.sync, nc.sync, nc.sync])
        w2_tile = load_words(w2_words, R, "w2_tile", nc.sync)
        load_plane(w2_plane, w2_scales, [nc.sync])
        list2 = load_list(offs2, "list2")
        list3 = load_list(offs3, "list3")

        pw = [sb.tile([P, C], F32, name="pw%d" % t) for t in range(3)]
        pv = [sb.tile([P, C], F32, name="pv%d" % t) for t in range(2)]
        for page in pw + pv:
            nc.vector.memset(page[:], 0.0)
        ws_plane = zeroed_plane(N, "ws_plane")
        sx_plane = zeroed_plane(O, "sx_plane")
        wb_plane = zeroed_plane(N, "wb_plane")

        list4 = load_list(offs4, "list4")
        list5 = load_list(offs5, "list5")
        tz_tiles = []
        for u in range(N // P):
            tile = sb.tile([P, E], F32, name="tz%d" % u)
            nc.sync.dma_start(tile[:], tz[u * P : (u + 1) * P, :])
            tz_tiles.append(tile)
        ws_tile = load_words(ws_words, N, "ws_tile", nc.sync)
        sx_tile = load_words(sx_words, O, "sx_tile", nc.sync)
        wb_tile = load_words(wb_words, N, "wb_tile", nc.sync)
        load_plane(ws_plane, ws_scales, [nc.sync])
        load_plane(sx_plane, sx_scales, [nc.sync])
        load_plane(wb_plane, wb_scales, [nc.sync])

        xg_words = sb.tile([P, J], U16, name="xg_words", align_bytes=64)
        xg_plane = sb.tile([P, J], U8, name="xg_plane", align_bytes=64)
        nc.vector.tensor_copy(xg_words[:], xt_tile[:].indirect(list1[:]))
        nc.vector.tensor_copy(xg_plane[:], xt_plane[:].indirect(list1[:]))

        def deal(words, plane, name):
            dealt_words = sb.tile([P, PACK, P], U32, name=name + "_dw", align_bytes=64)
            dealt_plane = sb.tile([P, PACK, P], U8, name=name + "_dp", align_bytes=64)
            nc.scalar.copy(
                dealt_words[:].rearrange("p t (c i) -> p c t i", i=4),
                words[:].rearrange("p (c i t) -> p c t i", i=4, t=PACK))
            nc.vector.tensor_copy(dealt_plane[:], plane[:].rearrange("p (m t) -> p t m", t=PACK))
            return dealt_words, dealt_plane

        dealt = [deal(w_tile, w_plane, "a"), deal(w2_tile, w2_plane, "b")]
        formats = [E5M2, E4M3]

        def first_stage(dst, m, t):
            nc.tensor.matmul_mx(
                out=dst, lhsT=dealt[m][0][:, t, :].bitcast(formats[m]), lhsT_scale=dealt[m][1][:, t, :],
                rhs=xg_words[:].bitcast(E2M1), rhs_scale=xg_plane[:], start=True, stop=True)

        a_banks = [ps.tile([P, 2, J], F32, name="a_bank%d" % h) for h in range(2)]
        b_lone = [ps.tile([P, J], F32, name="b_lone%d" % t) for t in range(2)]
        b_bank = ps.tile([P, 2, J], F32, name="b_bank")
        for t in range(2):
            first_stage(a_banks[0][:, t, :], 0, t)
        for t in range(2):
            first_stage(b_lone[t][:], 1, t)
        for t in range(2):
            first_stage(a_banks[1][:, t, :], 0, 2 + t)
        for t in range(2):
            first_stage(b_bank[:, t, :], 1, 2 + t)

        H = O // 2
        out_banks = []
        for h in range(2):
            bank = ps.tile([P, N // P, H], F32, name="out_bank%d" % h)
            reads = slice(h * H, (h + 1) * H)
            for u in range(N // P):
                cols = slice(u * P, (u + 1) * P)
                nc.tensor.matmul_mx(
                    out=bank[:, u, :], lhsT=ws_tile[:, cols].bitcast(E4M3), lhsT_scale=ws_plane[:, cols],
                    rhs=sx_tile[:, reads].bitcast(E5M2), rhs_scale=sx_plane[:, reads], start=(u == 0), stop=False)
            out_banks.append(bank)

        a_sb = sb.tile([P, PACK, J], F32, name="a_sb", tag="w2_plane", align_bytes=64)
        for h in range(2):
            nc.vector.tensor_copy(a_sb[:, 2 * h : 2 * h + 2, :], a_banks[h][:])
        b_first = sb.tile([P, J], F32, name="b_first", tag="b_shared")
        b_second = sb.tile([P, J], F32, name="b_second")
        nc.scalar.copy(b_first[:], b_lone[0][:])
        nc.scalar.copy(b_second[:], b_lone[1][:])
        b_sums = [b_first[:], b_second[:]]

        hid = sb.tile([P, PACK, O], F32, name="hid")
        pg = []
        for t in range(PACK):
            nc.vector.tensor_copy(pw[t % 3][:].indirect(list2[:]), a_sb[:, t, :])
            nc.scalar.activation(pv[t % 2][:].indirect(list3[:]), b_sums[t], COPY)
            if t == 0:
                b_rest = sb.tile([P, 2, J], F32, name="b_rest", tag="b_shared")
                nc.scalar.copy(b_rest[:], b_bank[:])
                b_sums.extend([b_rest[:, 0, :], b_rest[:, 1, :]])
            if t < PACK - 1:
                board = sb.tile([P, C], F32, name="pg%d" % t, tag="pg%d" % t)
                nc.gpsimd.tensor_tensor(board[:], pw[t % 3][:], pv[t % 2][:], ADD)
                pg.append(board)
        for t in range(2):
            nc.vector.tensor_copy(hid[:, t, :], pg[t][:].indirect(list4[:]))
        nc.scalar.activation(hid[:, 2, :], pg[2][:].indirect(list4[:]), COPY)
        board = sb.tile([P, C], F32, name="pg3", tag="pg1")
        nc.vector.tensor_tensor(board[:], pw[0][:], pv[1][:], ADD)
        nc.vector.tensor_copy(hid[:, 3, :H], board[:].indirect(list4[:, :8]))
        nc.scalar.activation(hid[:, 3, H:], board[:].indirect(list4[:, 8:]), COPY)

        picked = sb.tile([P, N // P, O], F32, name="picked", tag="pg1")
        for u in range(N // P):
            nc.scalar.activation(picked[:, u, :], tz_tiles[u][:].indirect(list5[:]), COPY)

        grouped = [sb.tile([P, H, PACK], BF16, name="grouped%d" % h, align_bytes=64) for h in range(2)]
        for h in range(2):
            nc.vector.tensor_copy(
                grouped[h][:].rearrange("p (c i) t -> p c t i", i=4),
                hid[:, :, h * H : (h + 1) * H].rearrange("p t (c i) -> p c t i", i=4))
        hid_words = [sb.tile([P, H], U32, name="hid_words%d" % h, align_bytes=64) for h in range(2)]
        hid_plane = [sb.tile([P, H], U8, name="hid_plane%d" % h, align_bytes=64) for h in range(2)]
        for h in range(2):
            nc.vector.quantize_mx(
                out=hid_words[h][:].bitcast(E5M2), scales=hid_plane[h][:],
                in_=grouped[h][:].rearrange("p o t -> p (o t)"))
        out_view = out.rearrange("(u p) o -> p u o", p=P)
        for h in range(2):
            reads = slice(h * H, (h + 1) * H)
            for u in range(N // P):
                cols = slice(u * P, (u + 1) * P)
                nc.tensor.matmul_mx(
                    out=out_banks[h][:, u, :], lhsT=wb_tile[:, cols].bitcast(E4M3), lhsT_scale=wb_plane[:, cols],
                    rhs=hid_words[h][:].bitcast(E5M2), rhs_scale=hid_plane[h][:], start=False, stop=(u == N // P - 1))
            result = sb.tile([P, N // P, H], F32, name="result%d" % h)
            nc.vector.tensor_tensor(result[:], out_banks[h][:], picked[:, :, reads], ADD)
            (nc.sync if h == 0 else nc.scalar).dma_start(out_view[:, :, reads], result[:])
